import numpy as np
import ml_dtypes


def mxq(x, axis, fmt="e4m3"):
    dtype, down = {"e4m3": (ml_dtypes.float8_e4m3fn, 7), "e5m2": (ml_dtypes.float8_e5m2, 14)}[fmt]
    v = np.moveaxis(np.asarray(x, np.float32).astype(ml_dtypes.bfloat16).astype(np.float64), axis, -1)
    blocks = v.reshape(v.shape[:-1] + (-1, 32))
    amax = np.abs(blocks).max(-1, keepdims=True)
    byte = np.maximum(np.where(amax > 0, np.frexp(amax)[1] - 1 + 127, 0) - down, 1)
    scale = np.exp2(byte - 127.0)
    codes = (blocks / scale).astype(np.float32).astype(dtype).astype(np.float64)
    return np.moveaxis((codes * scale).reshape(v.shape), -1, axis)


WIDE = False


def mx_kscale(k):
    if not WIDE:
        return np.ones(k)
    levels = np.array([10, -10, 5, -5, 0])
    if k % 512:
        return np.exp2(np.random.permutation(np.resize(levels, k // 32))).repeat(32)
    a = np.empty((k // 512, 16))
    for p in range(k // 512):
        a[p, :8] = np.random.permutation(np.resize(levels, 8))
        for g in range(8):
            far = levels[np.abs(levels - a[p, g]) >= 10]
            a[p, g + 8] = far[np.random.randint(len(far))]
    return np.exp2(a.ravel()).repeat(32)


def f64(x):
    return np.asarray(x).astype(np.float64)


def striped8(idx):
    return np.asarray(idx).reshape(8, -1, 16).transpose(0, 2, 1).reshape(128, -1).astype(np.uint16)


def unstriped8(offs):
    return offs.reshape(8, 16, -1).transpose(0, 2, 1).reshape(8, -1).astype(np.int64)


def pick8(x, idx, run):
    r = np.arange(len(x))
    return x[r[:, None], idx[r % (8 * run) // run]]


E2M1 = np.array([0.0, 0.5, 1.0, 1.5, 2.0, 3.0, 4.0, 6.0, -0.0, -0.5, -1.0, -1.5, -2.0, -3.0, -4.0, -6.0])


def pack_weight(w, fmt):
    k, n = w.shape
    w = f64(np.asarray(w, np.float32).astype(ml_dtypes.bfloat16)).reshape(k // 32, 32, n)
    amax = np.abs(w).max(1)
    if fmt == "e4m3":
        byte = np.frexp(amax)[1] - 1 + 127 - 7
    else:
        mant, ex = np.frexp(amax / 6.0)
        byte = np.where(mant > 0.5, ex, ex - 1) + 127
    byte = np.clip(np.where(amax > 0, byte, 1), 1, 254)
    scaled = (w * np.exp2(127.0 - byte)[:, None, :]).reshape(k, n).astype(np.float32)
    by_word = np.ascontiguousarray(scaled.reshape(k // 512, 128, 4, n).transpose(0, 1, 3, 2))
    if fmt == "e4m3":
        words = by_word.astype(ml_dtypes.float8_e4m3fn).view(np.uint8)
    else:
        c = by_word.astype(ml_dtypes.float4_e2m1fn).view(np.uint8) & 0xF
        words = (c[..., 0::2] | (c[..., 1::2] << 4)).reshape(k // 512, 128, 2 * n)
    return np.ascontiguousarray(words), np.ascontiguousarray(byte.astype(np.uint8).reshape(k // 512, 16, n))


def unpack_weight(words, scales, fmt):
    g, _, n = scales.shape
    words = np.ascontiguousarray(words).reshape(g, 128, n, -1)
    if fmt == "e4m3":
        vals = words.view(ml_dtypes.float8_e4m3fn).astype(np.float64)
    else:
        nib = np.empty((g, 128, n, 4), np.uint8)
        nib[..., 0::2] = words & 0xF
        nib[..., 1::2] = words >> 4
        vals = E2M1[nib]
    vals = vals * np.repeat(np.exp2(scales.astype(np.float64) - 127.0), 8, axis=1)[..., None]
    return vals.transpose(0, 1, 3, 2).reshape(g * 512, n)


D, E, T, Q, I = 512, 512, 1024, 128, 512


def setup_inputs():
    n = np.random.standard_normal
    idx = np.stack([np.random.permutation(T)[:I] for _ in range(8)])
    idx2 = np.stack([np.random.permutation(T)[:I] for _ in range(8)])
    fd = mx_kscale(D)
    fe = mx_kscale(E)
    keysp = pack_weight(n((D, T)) / fd[:, None], "e2m1")
    return {
        "query": (n((D, Q)) * 0.6 / np.sqrt(D) * fd[:, None]).astype(np.float32),
        "keys_words": keysp[0],
        "keys_scales": keysp[1],
        "gout": (n((E, Q)) * 1 / np.sqrt(E) * fe[:, None]).astype(np.float32),
        "vals": (n((E, T)) / fe[:, None]).astype(np.float32),
        "old": (0.5 * n((Q, T))).astype(np.float32),
        "offs": striped8(idx),
        "offs2": striped8(idx2),
    }


def reference(query, keys_words, keys_scales, gout, vals, old, offs, offs2):
    idx = unstriped8(offs)
    idx2 = unstriped8(offs2)
    keysu = unpack_weight(keys_words, keys_scales, "e2m1")
    queryq = mxq(f64(query), 0, "e4m3")
    a = queryq.T @ keysu
    goutq = mxq(f64(gout), 0, "e4m3")
    valsq = mxq(f64(vals), 0, "e4m3")
    dw = goutq.T @ valsq
    p = np.exp(pick8(a, idx, 16) - np.max(pick8(a, idx, 16), axis=1, keepdims=True))
    w = p / np.sum(p, axis=1, keepdims=True) * 512.0
    mw = np.sum(w * pick8(dw, idx2, 16), axis=1, keepdims=True) / 512.0
    ds = w * (pick8(dw, idx2, 16) - mw)
    df = np.zeros((Q, T))
    df[np.arange(Q)[:, None], idx[np.arange(Q) % 128 // 16]] = ds
    y = f64(old) + df
    return y

@@ -1,0 +1,156 @@
+from contextlib import ExitStack
+
+import concourse.mybir as mybir
+
+D, E, T, Q, I = 512, 512, 1024, 128, 512
+FLOPS = 2 * D * Q * T + 2 * E * Q * T
+
+F32 = mybir.dt.float32
+BF16 = mybir.dt.bfloat16
+I32 = mybir.dt.int32
+U32 = mybir.dt.uint32
+U16 = mybir.dt.uint16
+U8 = mybir.dt.uint8
+FP8X4 = mybir.dt.float8_e4m3fn_x4
+FP4X4 = mybir.dt.float4_e2m1fn_x4
+ALU = mybir.AluOpType
+ACT = mybir.ActivationFunctionType
+
+P = 128
+PACK = 4
+BANK = 512
+CHUNKS = (256, 256, 256, 128, 128)
+SCALAR_COLS = (256, 128, 160, 64, 48)
+OUT_CHUNKS = (256, 256, 256, 256)
+
+
+def weave(copy, grouped, raw, c0, c1):
+    copy(
+        out=grouped[:, PACK * c0 : PACK * c1].rearrange("p (c i t) -> p c t i", i=4, t=PACK),
+        in_=raw[:, :, c0:c1].rearrange("p t (c i) -> p c t i", i=4),
+    )
+
+
+def tile_attend_gfollow_heads_kernel(tc, query, keys_words, keys_scales, gout, vals, old, offs, offs2, out):
+    nc = tc.nc
+    with ExitStack() as ctx:
+        keep = ctx.enter_context(tc.tile_pool(name="keep", bufs=1))
+        psum = ctx.enter_context(tc.psum_pool(name="psum", bufs=1))
+
+        k_scales = keep.tile([P, T], U8, align_bytes=64)
+        nc.vector.memset(k_scales[:].bitcast(I32), 0)
+        df = keep.tile([P, T], F32)
+        nc.gpsimd.memset(df[:], 0.0)
+        warm_in = keep.tile([P, 1], F32)
+        nc.gpsimd.memset(warm_in[:], 0.0)
+        warm_out = keep.tile([P, 1], F32)
+        nc.scalar.activation(out=warm_out[:], in_=warm_in[:], func=ACT.Exp)
+
+        q_raw = keep.tile([P, PACK, Q], F32)
+        nc.sync.dma_start(out=q_raw[:], in_=query.rearrange("(p t) q -> p t q", t=PACK))
+        k_words = keep.tile([P, 2 * T], U8, align_bytes=64)
+        nc.sync.dma_start(out=k_words[:].bitcast(I32), in_=keys_words[0].bitcast(I32))
+        for quad in range(4):
+            nc.sync.dma_start(
+                out=k_scales[32 * quad : 32 * quad + 4, :].bitcast(I32),
+                in_=keys_scales[0, 4 * quad : 4 * quad + 4, :].bitcast(I32),
+            )
+        lists = keep.tile([P, I // 16], U16)
+        nc.sync.dma_start(lists[:], offs)
+        g_raw = keep.tile([P, PACK, Q], F32)
+        nc.sync.dma_start(out=g_raw[:], in_=gout.rearrange("(p t) q -> p t q", t=PACK))
+        vals_by_word = vals.rearrange("(p t) c -> p t c", t=PACK)
+        v_raw = []
+        c0 = 0
+        for n, width in enumerate(CHUNKS):
+            raw = keep.tile([P, PACK, width], F32, name=f"v_raw{n}")
+            nc.sync.dma_start(out=raw[:], in_=vals_by_word[:, :, c0 : c0 + width])
+            v_raw.append(raw)
+            c0 = c0 + width
+        lists2 = keep.tile([P, I // 16], U16)
+        nc.sync.dma_start(lists2[:], offs2)
+        old_sb = keep.tile([P, T], F32)
+        nc.sync.dma_start(out=old_sb[:], in_=old)
+
+        q_bf = keep.tile([P, PACK * Q], BF16, align_bytes=64)
+        weave(nc.vector.tensor_copy, q_bf, q_raw, 0, Q)
+        q_codes = keep.tile([P, Q], U32, align_bytes=64)
+        q_scales = keep.tile([P, Q], U8, align_bytes=64)
+        nc.vector.quantize_mx(out=q_codes[:].bitcast(FP8X4), scales=q_scales[:], in_=q_bf[:])
+        scores = keep.tile([P, T], F32)
+        for half, copy in enumerate((nc.scalar.copy, nc.vector.tensor_copy)):
+            bank = psum.tile([P, BANK], F32, name=f"score_bank{half}")
+            cols = slice(half * BANK, (half + 1) * BANK)
+            nc.tensor.matmul_mx(
+                out=bank[:],
+                lhsT=q_codes[:].bitcast(FP8X4),
+                lhsT_scale=q_scales[:],
+                rhs=k_words[:, 2 * cols.start : 2 * cols.stop].bitcast(FP4X4),
+                rhs_scale=k_scales[:, cols],
+                start=True,
+                stop=True,
+            )
+            copy(out=scores[:, cols], in_=bank[:])
+
+        g_bf = keep.tile([P, PACK * Q], BF16, align_bytes=64)
+        weave(nc.scalar.copy, g_bf, g_raw, 0, Q)
+        g_codes = keep.tile([P, Q], U32, align_bytes=64)
+        g_scales = keep.tile([P, Q], U8, align_bytes=64)
+        nc.vector.quantize_mx(out=g_codes[:].bitcast(FP8X4), scales=g_scales[:], in_=g_bf[:])
+
+        listed = keep.tile([P, I], F32)
+        nc.vector.tensor_copy(out=listed[:], in_=scores[:].indirect(lists[:]))
+        neg_max = keep.tile([P, 1], F32)
+        nc.vector.tensor_reduce(out=neg_max[:], in_=listed[:], axis=mybir.AxisListType.X, op=ALU.max, negate=True)
+        p = keep.tile([P, I], F32)
+        p_sum = keep.tile([P, 1], F32)
+        nc.scalar.activation(out=p[:], in_=listed[:], func=ACT.Exp, bias=neg_max[:], accum_out=p_sum[:])
+        inv_sum = keep.tile([P, 1], F32)
+        nc.vector.reciprocal(out=inv_sum[:], in_=p_sum[:])
+        gain = keep.tile([P, 1], F32)
+        nc.vector.tensor_scalar(out=gain[:], in0=inv_sum[:], scalar1=float(I), scalar2=None, op0=ALU.mult)
+
+        dw = keep.tile([P, T], F32)
+        c0 = 0
+        for n, width in enumerate(CHUNKS):
+            v_bf = keep.tile([P, PACK * width], BF16, align_bytes=64, name=f"v_bf{n}")
+            share = SCALAR_COLS[n]
+            weave(nc.scalar.copy, v_bf, v_raw[n], 0, share)
+            if share < width:
+                weave(nc.vector.tensor_copy, v_bf, v_raw[n], share, width)
+            v_codes = keep.tile([P, width], U32, align_bytes=64, name=f"v_codes{n}")
+            v_scales = keep.tile([P, width], U8, align_bytes=64, name=f"v_scales{n}")
+            nc.vector.quantize_mx(out=v_codes[:].bitcast(FP8X4), scales=v_scales[:], in_=v_bf[:])
+            bank = psum.tile([P, width], F32, name=f"dw_bank{n}")
+            nc.tensor.matmul_mx(
+                out=bank[:],
+                lhsT=g_codes[:].bitcast(FP8X4),
+                lhsT_scale=g_scales[:],
+                rhs=v_codes[:].bitcast(FP8X4),
+                rhs_scale=v_scales[:],
+                start=True,
+                stop=True,
+            )
+            nc.scalar.copy(out=dw[:, c0 : c0 + width], in_=bank[:])
+            c0 = c0 + width
+
+        moved = keep.tile([P, I], F32)
+        nc.vector.tensor_copy(out=moved[:], in_=dw[:].indirect(lists2[:]))
+        prod = keep.tile([P, I], F32)
+        mean = keep.tile([P, 1], F32)
+        nc.vector.scalar_tensor_tensor(
+            out=prod[:], in0=moved[:], scalar=inv_sum[:], in1=p[:], op0=ALU.mult, op1=ALU.mult, accum_out=mean[:]
+        )
+        centred = keep.tile([P, I], F32)
+        nc.vector.tensor_scalar(
+            out=centred[:], in0=moved[:], scalar1=mean[:], scalar2=gain[:], op0=ALU.subtract, op1=ALU.mult
+        )
+        nc.vector.tensor_tensor(out=df[:].indirect(lists[:]), in0=centred[:], in1=p[:], op=ALU.mult)
+        c0 = 0
+        for n, width in enumerate(OUT_CHUNKS):
+            res = keep.tile([P, width], F32, name=f"res{n}")
+            cols = slice(c0, c0 + width)
+            nc.vector.tensor_tensor(out=res[:], in0=df[:, cols], in1=old_sb[:, cols], op=ALU.add)
+            queue = nc.sync if n % 2 == 0 else nc.scalar
+            queue.dma_start(out=out[:, cols], in_=res[:])
+            c0 = c0 + width

@@ -19,15 +19,16 @@ ACT = mybir.ActivationFunctionType
 P = 128
 PACK = 4
 BANK = 512
-CHUNKS = (256, 256, 256, 128, 128)
-SCALAR_COLS = (256, 128, 160, 64, 48)
+CHUNK = 256
+HALF = I // 2
+SCALAR_COLS = (0, 256, 128)
 OUT_CHUNKS = (256, 256, 256, 256)
 
 
-def weave(copy, grouped, raw, c0, c1):
+def weave(copy, grouped, raw):
     copy(
-        out=grouped[:, PACK * c0 : PACK * c1].rearrange("p (c i t) -> p c t i", i=4, t=PACK),
-        in_=raw[:, :, c0:c1].rearrange("p t (c i) -> p c t i", i=4),
+        out=grouped.rearrange("p (c i t) -> p c t i", i=4, t=PACK),
+        in_=raw.rearrange("p t (c i) -> p c t i", i=4),
     )
 
 
@@ -37,14 +38,27 @@ def tile_attend_gfollow_heads_kernel(tc, query, keys_words, keys_scales, gout, v
         keep = ctx.enter_context(tc.tile_pool(name="keep", bufs=1))
         psum = ctx.enter_context(tc.psum_pool(name="psum", bufs=1))
 
+        def quantize(bf, width, name):
+            codes = keep.tile([P, width], U32, align_bytes=64, name=f"{name}_codes")
+            scales = keep.tile([P, width], U8, align_bytes=64, name=f"{name}_scales")
+            nc.vector.quantize_mx(out=codes[:].bitcast(FP8X4), scales=scales[:], in_=bf[:])
+            return codes, scales
+
         k_scales = keep.tile([P, T], U8, align_bytes=64)
         nc.vector.memset(k_scales[:].bitcast(I32), 0)
-        df = keep.tile([P, T], F32)
-        nc.gpsimd.memset(df[:], 0.0)
         warm_in = keep.tile([P, 1], F32)
         nc.gpsimd.memset(warm_in[:], 0.0)
+        df = keep.tile([P, T], F32)
+        nc.gpsimd.memset(df[:], 0.0)
         warm_out = keep.tile([P, 1], F32)
         nc.scalar.activation(out=warm_out[:], in_=warm_in[:], func=ACT.Exp)
+
+        chunks = T // CHUNK
+        vals_by_word = vals.rearrange("(p t) c -> p t c", t=PACK)
+        v_raw = [keep.tile([P, PACK, CHUNK], F32, name=f"v_raw{n}") for n in range(chunks)]
+
+        def load_vals(n):
+            nc.sync.dma_start(out=v_raw[n][:], in_=vals_by_word[:, :, n * CHUNK : (n + 1) * CHUNK])
 
         q_raw = keep.tile([P, PACK, Q], F32)
         nc.sync.dma_start(out=q_raw[:], in_=query.rearrange("(p t) q -> p t q", t=PACK))
@@ -55,30 +69,23 @@ def tile_attend_gfollow_heads_kernel(tc, query, keys_words, keys_scales, gout, v
                 out=k_scales[32 * quad : 32 * quad + 4, :].bitcast(I32),
                 in_=keys_scales[0, 4 * quad : 4 * quad + 4, :].bitcast(I32),
             )
-        lists = keep.tile([P, I // 16], U16)
-        nc.sync.dma_start(lists[:], offs)
         g_raw = keep.tile([P, PACK, Q], F32)
         nc.sync.dma_start(out=g_raw[:], in_=gout.rearrange("(p t) q -> p t q", t=PACK))
-        vals_by_word = vals.rearrange("(p t) c -> p t c", t=PACK)
-        v_raw = []
-        c0 = 0
-        for n, width in enumerate(CHUNKS):
-            raw = keep.tile([P, PACK, width], F32, name=f"v_raw{n}")
-            nc.sync.dma_start(out=raw[:], in_=vals_by_word[:, :, c0 : c0 + width])
-            v_raw.append(raw)
-            c0 = c0 + width
+        load_vals(0)
+        lists = keep.tile([P, I // 16], U16)
+        nc.sync.dma_start(lists[:], offs)
+        for n in range(1, chunks):
+            load_vals(n)
         lists2 = keep.tile([P, I // 16], U16)
         nc.sync.dma_start(lists2[:], offs2)
         old_sb = keep.tile([P, T], F32)
         nc.sync.dma_start(out=old_sb[:], in_=old)
 
         q_bf = keep.tile([P, PACK * Q], BF16, align_bytes=64)
-        weave(nc.vector.tensor_copy, q_bf, q_raw, 0, Q)
-        q_codes = keep.tile([P, Q], U32, align_bytes=64)
-        q_scales = keep.tile([P, Q], U8, align_bytes=64)
-        nc.vector.quantize_mx(out=q_codes[:].bitcast(FP8X4), scales=q_scales[:], in_=q_bf[:])
+        weave(nc.vector.tensor_copy, q_bf[:], q_raw[:])
+        q_codes, q_scales = quantize(q_bf, Q, "q")
         scores = keep.tile([P, T], F32)
-        for half, copy in enumerate((nc.scalar.copy, nc.vector.tensor_copy)):
+        for half in range(2):
             bank = psum.tile([P, BANK], F32, name=f"score_bank{half}")
             cols = slice(half * BANK, (half + 1) * BANK)
             nc.tensor.matmul_mx(
@@ -90,52 +97,61 @@ def tile_attend_gfollow_heads_kernel(tc, query, keys_words, keys_scales, gout, v
                 start=True,
                 stop=True,
             )
-            copy(out=scores[:, cols], in_=bank[:])
+            nc.scalar.copy(out=scores[:, cols], in_=bank[:])
 
         g_bf = keep.tile([P, PACK * Q], BF16, align_bytes=64)
-        weave(nc.scalar.copy, g_bf, g_raw, 0, Q)
-        g_codes = keep.tile([P, Q], U32, align_bytes=64)
-        g_scales = keep.tile([P, Q], U8, align_bytes=64)
-        nc.vector.quantize_mx(out=g_codes[:].bitcast(FP8X4), scales=g_scales[:], in_=g_bf[:])
+        weave(nc.vector.tensor_copy, g_bf[:], g_raw[:])
+        g_codes, g_scales = quantize(g_bf, Q, "g")
 
         listed = keep.tile([P, I], F32)
         nc.vector.tensor_copy(out=listed[:], in_=scores[:].indirect(lists[:]))
-        neg_max = keep.tile([P, 1], F32)
-        nc.vector.tensor_reduce(out=neg_max[:], in_=listed[:], axis=mybir.AxisListType.X, op=ALU.max, negate=True)
-        p = keep.tile([P, I], F32)
-        p_sum = keep.tile([P, 1], F32)
-        nc.scalar.activation(out=p[:], in_=listed[:], func=ACT.Exp, bias=neg_max[:], accum_out=p_sum[:])
-        inv_sum = keep.tile([P, 1], F32)
-        nc.vector.reciprocal(out=inv_sum[:], in_=p_sum[:])
-        gain = keep.tile([P, 1], F32)
-        nc.vector.tensor_scalar(out=gain[:], in0=inv_sum[:], scalar1=float(I), scalar2=None, op0=ALU.mult)
 
-        dw = keep.tile([P, T], F32)
-        c0 = 0
-        for n, width in enumerate(CHUNKS):
-            v_bf = keep.tile([P, PACK * width], BF16, align_bytes=64, name=f"v_bf{n}")
-            share = SCALAR_COLS[n]
-            weave(nc.scalar.copy, v_bf, v_raw[n], 0, share)
-            if share < width:
-                weave(nc.vector.tensor_copy, v_bf, v_raw[n], share, width)
-            v_codes = keep.tile([P, width], U32, align_bytes=64, name=f"v_codes{n}")
-            v_scales = keep.tile([P, width], U8, align_bytes=64, name=f"v_scales{n}")
-            nc.vector.quantize_mx(out=v_codes[:].bitcast(FP8X4), scales=v_scales[:], in_=v_bf[:])
-            bank = psum.tile([P, width], F32, name=f"dw_bank{n}")
+        def product(bank_cols, codes, scales):
             nc.tensor.matmul_mx(
-                out=bank[:],
+                out=bank_cols,
                 lhsT=g_codes[:].bitcast(FP8X4),
                 lhsT_scale=g_scales[:],
-                rhs=v_codes[:].bitcast(FP8X4),
-                rhs_scale=v_scales[:],
+                rhs=codes[:].bitcast(FP8X4),
+                rhs_scale=scales[:],
                 start=True,
                 stop=True,
             )
-            nc.scalar.copy(out=dw[:, c0 : c0 + width], in_=bank[:])
-            c0 = c0 + width
+
+        early_bank = psum.tile([P, BANK], F32)
+        third_bank = psum.tile([P, CHUNK], F32)
+        targets = (early_bank[:, :CHUNK], early_bank[:, CHUNK:], third_bank[:])
+        p = keep.tile([P, I], F32)
+        p_sum = keep.tile([P, 1], F32)
+        for n in range(chunks - 1):
+            v_bf = keep.tile([P, PACK * CHUNK], BF16, align_bytes=64, name=f"v_bf{n}")
+            share = SCALAR_COLS[n]
+            if share > 0:
+                weave(nc.scalar.copy, v_bf[:, : PACK * share], v_raw[n][:, :, :share])
+            if share < CHUNK:
+                weave(nc.vector.tensor_copy, v_bf[:, PACK * share :], v_raw[n][:, :, share:])
+            product(targets[n], *quantize(v_bf, CHUNK, f"v{n}"))
+        last = []
+        for h, copy in enumerate((nc.vector.tensor_copy, nc.scalar.copy)):
+            v_bf = keep.tile([P, PACK * CHUNK // 2], BF16, align_bytes=64, name=f"v_last{h}")
+            weave(copy, v_bf[:], v_raw[-1][:, :, h * CHUNK // 2 : (h + 1) * CHUNK // 2])
+            bank = psum.tile([P, CHUNK // 2], F32, name=f"last_bank{h}")
+            product(bank[:], *quantize(v_bf, CHUNK // 2, f"v_last{h}"))
+            last.append(bank)
+
+        neg_max = keep.tile([P, 1], F32, align_bytes=64, tag="v_last1")
+        nc.vector.tensor_reduce(out=neg_max[:], in_=listed[:], axis=mybir.AxisListType.X, op=ALU.max, negate=True)
+
+        dw = keep.tile([P, T], F32, tag=f"v_raw{chunks - 1}")
+        nc.scalar.copy(out=dw[:, :BANK], in_=early_bank[:])
+        nc.scalar.copy(out=dw[:, BANK : BANK + CHUNK], in_=third_bank[:])
+        nc.vector.tensor_copy(out=dw[:, T - CHUNK : T - CHUNK // 2], in_=last[0][:])
+        nc.scalar.copy(out=dw[:, T - CHUNK // 2 :], in_=last[1][:])
+        nc.scalar.activation(out=p[:], in_=listed[:], func=ACT.Exp, bias=neg_max[:], accum_out=p_sum[:])
 
         moved = keep.tile([P, I], F32)
         nc.vector.tensor_copy(out=moved[:], in_=dw[:].indirect(lists2[:]))
+        inv_sum = keep.tile([P, 1], F32, tag=f"v_raw{chunks - 1}")
+        nc.vector.reciprocal(out=inv_sum[:], in_=p_sum[:])
         prod = keep.tile([P, I], F32)
         mean = keep.tile([P, 1], F32)
         nc.vector.scalar_tensor_tensor(
@@ -143,14 +159,16 @@ def tile_attend_gfollow_heads_kernel(tc, query, keys_words, keys_scales, gout, v
         )
         centred = keep.tile([P, I], F32)
         nc.vector.tensor_scalar(
-            out=centred[:], in0=moved[:], scalar1=mean[:], scalar2=gain[:], op0=ALU.subtract, op1=ALU.mult
+            out=centred[:], in0=moved[:], scalar1=mean[:], scalar2=inv_sum[:], op0=ALU.subtract, op1=ALU.mult
         )
         nc.vector.tensor_tensor(out=df[:].indirect(lists[:]), in0=centred[:], in1=p[:], op=ALU.mult)
         c0 = 0
         for n, width in enumerate(OUT_CHUNKS):
             res = keep.tile([P, width], F32, name=f"res{n}")
             cols = slice(c0, c0 + width)
-            nc.vector.tensor_tensor(out=res[:], in0=df[:, cols], in1=old_sb[:, cols], op=ALU.add)
+            nc.vector.scalar_tensor_tensor(
+                out=res[:], in0=df[:, cols], scalar=float(I), in1=old_sb[:, cols], op0=ALU.mult, op1=ALU.add
+            )
             queue = nc.sync if n % 2 == 0 else nc.scalar
             queue.dma_start(out=out[:, cols], in_=res[:])
             c0 = c0 + width

@@ -19,9 +19,9 @@ ACT = mybir.ActivationFunctionType
 P = 128
 PACK = 4
 BANK = 512
-CHUNK = 256
-HALF = I // 2
-SCALAR_COLS = (0, 256, 128)
+CHUNKS = (384, 384, 256)
+PIECES = (((0, 128), (128, 384)), ((256, 384), (0, 256)), ((128, 256), (0, 128)))
+SCALAR_COLS = (384, 192, 128)
 OUT_CHUNKS = (256, 256, 256, 256)
 
 
@@ -41,25 +41,27 @@ def tile_attend_gfollow_heads_kernel(tc, query, keys_words, keys_scales, gout, v
         def quantize(bf, width, name):
             codes = keep.tile([P, width], U32, align_bytes=64, name=f"{name}_codes")
             scales = keep.tile([P, width], U8, align_bytes=64, name=f"{name}_scales")
-            nc.vector.quantize_mx(out=codes[:].bitcast(FP8X4), scales=scales[:], in_=bf[:])
+            nc.vector.quantize_mx(out=codes[:].bitcast(FP8X4), scales=scales[:], in_=bf)
             return codes, scales
 
         k_scales = keep.tile([P, T], U8, align_bytes=64)
         nc.vector.memset(k_scales[:].bitcast(I32), 0)
         warm_in = keep.tile([P, 1], F32)
-        nc.gpsimd.memset(warm_in[:], 0.0)
+        nc.vector.memset(warm_in[:], 0.0)
         df = keep.tile([P, T], F32)
-        nc.gpsimd.memset(df[:], 0.0)
+        nc.vector.memset(df[:], 0.0)
         warm_out = keep.tile([P, 1], F32)
         nc.scalar.activation(out=warm_out[:], in_=warm_in[:], func=ACT.Exp)
 
-        chunks = T // CHUNK
+        starts = [sum(CHUNKS[:n]) for n in range(len(CHUNKS))]
         vals_by_word = vals.rearrange("(p t) c -> p t c", t=PACK)
-        v_raw = [keep.tile([P, PACK, CHUNK], F32, name=f"v_raw{n}") for n in range(chunks)]
+        v_raw = [keep.tile([P, PACK, width], F32, name=f"v_raw{n}") for n, width in enumerate(CHUNKS)]
 
         def load_vals(n):
-            nc.sync.dma_start(out=v_raw[n][:], in_=vals_by_word[:, :, n * CHUNK : (n + 1) * CHUNK])
+            nc.sync.dma_start(out=v_raw[n][:], in_=vals_by_word[:, :, starts[n] : starts[n] + CHUNKS[n]])
 
+        lists = keep.tile([P, I // 16], U16)
+        nc.sync.dma_start(lists[:], offs)
         q_raw = keep.tile([P, PACK, Q], F32)
         nc.sync.dma_start(out=q_raw[:], in_=query.rearrange("(p t) q -> p t q", t=PACK))
         k_words = keep.tile([P, 2 * T], U8, align_bytes=64)
@@ -72,9 +74,7 @@ def tile_attend_gfollow_heads_kernel(tc, query, keys_words, keys_scales, gout, v
         g_raw = keep.tile([P, PACK, Q], F32)
         nc.sync.dma_start(out=g_raw[:], in_=gout.rearrange("(p t) q -> p t q", t=PACK))
         load_vals(0)
-        lists = keep.tile([P, I // 16], U16)
-        nc.sync.dma_start(lists[:], offs)
-        for n in range(1, chunks):
+        for n in range(1, len(CHUNKS)):
             load_vals(n)
         lists2 = keep.tile([P, I // 16], U16)
         nc.sync.dma_start(lists2[:], offs2)
@@ -83,11 +83,12 @@ def tile_attend_gfollow_heads_kernel(tc, query, keys_words, keys_scales, gout, v
 
         q_bf = keep.tile([P, PACK * Q], BF16, align_bytes=64)
         weave(nc.vector.tensor_copy, q_bf[:], q_raw[:])
-        q_codes, q_scales = quantize(q_bf, Q, "q")
-        scores = keep.tile([P, T], F32)
-        for half in range(2):
-            bank = psum.tile([P, BANK], F32, name=f"score_bank{half}")
-            cols = slice(half * BANK, (half + 1) * BANK)
+        q_codes, q_scales = quantize(q_bf[:], Q, "q")
+        scores = keep.tile([P, T], F32, align_bytes=64)
+        c0 = 0
+        for n, (width, copy) in enumerate(((512, nc.scalar.copy), (256, nc.vector.tensor_copy), (256, nc.vector.tensor_copy))):
+            bank = psum.tile([P, width], F32, name=f"score_bank{n}")
+            cols = slice(c0, c0 + width)
             nc.tensor.matmul_mx(
                 out=bank[:],
                 lhsT=q_codes[:].bitcast(FP8X4),
@@ -97,16 +98,28 @@ def tile_attend_gfollow_heads_kernel(tc, query, keys_words, keys_scales, gout, v
                 start=True,
                 stop=True,
             )
-            nc.scalar.copy(out=scores[:, cols], in_=bank[:])
+            copy(out=scores[:, cols], in_=bank[:])
+            c0 = c0 + width
 
         g_bf = keep.tile([P, PACK * Q], BF16, align_bytes=64)
         weave(nc.vector.tensor_copy, g_bf[:], g_raw[:])
-        g_codes, g_scales = quantize(g_bf, Q, "g")
+        g_codes, g_scales = quantize(g_bf[:], Q, "g")
 
         listed = keep.tile([P, I], F32)
         nc.vector.tensor_copy(out=listed[:], in_=scores[:].indirect(lists[:]))
+        neg_max = keep.tile([P, 1], F32)
+        nc.vector.tensor_reduce(out=neg_max[:], in_=listed[:], axis=mybir.AxisListType.X, op=ALU.max, negate=True)
 
-        def product(bank_cols, codes, scales):
+        def cast(n, c0, c1, share, tag):
+            v_bf = keep.tile([P, PACK * (c1 - c0)], BF16, align_bytes=64, name=f"v_bf{n}_{c0}", tag=tag)
+            if share > 0:
+                weave(nc.scalar.copy, v_bf[:, : PACK * share], v_raw[n][:, :, c0 : c0 + share])
+            if c0 + share < c1:
+                weave(nc.vector.tensor_copy, v_bf[:, PACK * share :], v_raw[n][:, :, c0 + share : c1])
+            return v_bf
+
+        def product(v_bf, cols, bank_cols, name):
+            codes, scales = quantize(v_bf[:, PACK * cols.start : PACK * cols.stop], cols.stop - cols.start, name)
             nc.tensor.matmul_mx(
                 out=bank_cols,
                 lhsT=g_codes[:].bitcast(FP8X4),
@@ -117,41 +130,31 @@ def tile_attend_gfollow_heads_kernel(tc, query, keys_words, keys_scales, gout, v
                 stop=True,
             )
 
-        early_bank = psum.tile([P, BANK], F32)
-        third_bank = psum.tile([P, CHUNK], F32)
-        targets = (early_bank[:, :CHUNK], early_bank[:, CHUNK:], third_bank[:])
+        banks = [psum.tile([P, CHUNKS[n]], F32, name=f"dw_bank{n}") for n in range(2)]
+        product(cast(0, 0, 256, 256, "v_first"), slice(0, 256), banks[0][:, :256], "v0_0")
+        product(cast(0, 256, 384, 0, "scores"), slice(0, 128), banks[0][:, 256:], "v0_256")
         p = keep.tile([P, I], F32)
-        p_sum = keep.tile([P, 1], F32)
-        for n in range(chunks - 1):
-            v_bf = keep.tile([P, PACK * CHUNK], BF16, align_bytes=64, name=f"v_bf{n}")
-            share = SCALAR_COLS[n]
-            if share > 0:
-                weave(nc.scalar.copy, v_bf[:, : PACK * share], v_raw[n][:, :, :share])
-            if share < CHUNK:
-                weave(nc.vector.tensor_copy, v_bf[:, PACK * share :], v_raw[n][:, :, share:])
-            product(targets[n], *quantize(v_bf, CHUNK, f"v{n}"))
+        p_sum = v_raw[0][:, 0, 0:1]
+        nc.scalar.activation(out=p[:], in_=listed[:], func=ACT.Exp, bias=neg_max[:], accum_out=p_sum)
+        v_bf = cast(1, 0, 384, 192, "v_second")
+        product(v_bf, slice(256, 384), banks[1][:, 256:], "v1_256")
+        product(v_bf, slice(0, 256), banks[1][:, :256], "v1_0")
         last = []
-        for h, copy in enumerate((nc.vector.tensor_copy, nc.scalar.copy)):
-            v_bf = keep.tile([P, PACK * CHUNK // 2], BF16, align_bytes=64, name=f"v_last{h}")
-            weave(copy, v_bf[:], v_raw[-1][:, :, h * CHUNK // 2 : (h + 1) * CHUNK // 2])
-            bank = psum.tile([P, CHUNK // 2], F32, name=f"last_bank{h}")
-            product(bank[:], *quantize(v_bf, CHUNK // 2, f"v_last{h}"))
-            last.append(bank)
+        for c0, share, tag in ((128, 0, "v_second"), (0, 128, "v_last")):
+            bank = psum.tile([P, 128], F32, name=f"last_bank{c0}")
+            product(cast(2, c0, c0 + 128, share, tag), slice(0, 128), bank[:], f"v2_{c0}")
+            last.append((slice(starts[2] + c0, starts[2] + c0 + 128), bank))
+        inv_sum = keep.tile([P, 1], F32, align_bytes=64, tag="v_last")
+        nc.vector.reciprocal(out=inv_sum[:], in_=p_sum)
 
-        neg_max = keep.tile([P, 1], F32, align_bytes=64, tag="v_last1")
-        nc.vector.tensor_reduce(out=neg_max[:], in_=listed[:], axis=mybir.AxisListType.X, op=ALU.max, negate=True)
-
-        dw = keep.tile([P, T], F32, tag=f"v_raw{chunks - 1}")
-        nc.scalar.copy(out=dw[:, :BANK], in_=early_bank[:])
-        nc.scalar.copy(out=dw[:, BANK : BANK + CHUNK], in_=third_bank[:])
-        nc.vector.tensor_copy(out=dw[:, T - CHUNK : T - CHUNK // 2], in_=last[0][:])
-        nc.scalar.copy(out=dw[:, T - CHUNK // 2 :], in_=last[1][:])
-        nc.scalar.activation(out=p[:], in_=listed[:], func=ACT.Exp, bias=neg_max[:], accum_out=p_sum[:])
+        dw = keep.tile([P, T], F32, tag="v_raw2")
+        nc.scalar.copy(out=dw[:, : starts[1]], in_=banks[0][:])
+        nc.vector.tensor_copy(out=dw[:, starts[1] : starts[2]], in_=banks[1][:])
+        for (cols, bank), copy in zip(last, (nc.vector.tensor_copy, nc.scalar.copy)):
+            copy(out=dw[:, cols], in_=bank[:])
 
         moved = keep.tile([P, I], F32)
         nc.vector.tensor_copy(out=moved[:], in_=dw[:].indirect(lists2[:]))
-        inv_sum = keep.tile([P, 1], F32, tag=f"v_raw{chunks - 1}")
-        nc.vector.reciprocal(out=inv_sum[:], in_=p_sum[:])
         prod = keep.tile([P, I], F32)
         mean = keep.tile([P, 1], F32)
         nc.vector.scalar_tensor_tensor(

@@ -19,7 +19,7 @@ ACT = mybir.ActivationFunctionType
 P = 128
 PACK = 4
 BANK = 512
-CHUNKS = (384, 384, 256)
+CHUNKS = (256, 256, 256, 256)
 PIECES = (((0, 128), (128, 384)), ((256, 384), (0, 256)), ((128, 256), (0, 128)))
 SCALAR_COLS = (384, 192, 128)
 OUT_CHUNKS = (256, 256, 256, 256)
@@ -66,11 +66,8 @@ def tile_attend_gfollow_heads_kernel(tc, query, keys_words, keys_scales, gout, v
         nc.sync.dma_start(out=q_raw[:], in_=query.rearrange("(p t) q -> p t q", t=PACK))
         k_words = keep.tile([P, 2 * T], U8, align_bytes=64)
         nc.sync.dma_start(out=k_words[:].bitcast(I32), in_=keys_words[0].bitcast(I32))
-        for quad in range(4):
-            nc.sync.dma_start(
-                out=k_scales[32 * quad : 32 * quad + 4, :].bitcast(I32),
-                in_=keys_scales[0, 4 * quad : 4 * quad + 4, :].bitcast(I32),
-            )
+        for r in range(4):
+            nc.sync.dma_start(out=k_scales[r:P:32, :].bitcast(I32), in_=keys_scales[0, r:16:4, :].bitcast(I32))
         g_raw = keep.tile([P, PACK, Q], F32)
         nc.sync.dma_start(out=g_raw[:], in_=gout.rearrange("(p t) q -> p t q", t=PACK))
         load_vals(0)
@@ -130,28 +127,25 @@ def tile_attend_gfollow_heads_kernel(tc, query, keys_words, keys_scales, gout, v
                 stop=True,
             )
 
-        banks = [psum.tile([P, CHUNKS[n]], F32, name=f"dw_bank{n}") for n in range(2)]
-        product(cast(0, 0, 256, 256, "v_first"), slice(0, 256), banks[0][:, :256], "v0_0")
-        product(cast(0, 256, 384, 0, "scores"), slice(0, 128), banks[0][:, 256:], "v0_256")
+        first_bank = psum.tile([P, 512], F32)
+        third_bank = psum.tile([P, 256], F32)
+        last_banks = [psum.tile([P, 128], F32, name=f"last_bank{h}") for h in range(2)]
+        product(cast(0, 0, 256, 256, "v_first"), slice(0, 256), first_bank[:, :256], "v0")
+        product(cast(1, 0, 256, 256, "v_ring"), slice(0, 256), first_bank[:, 256:], "v1")
         p = keep.tile([P, I], F32)
-        p_sum = v_raw[0][:, 0, 0:1]
+        p_sum = v_raw[1][:, 0, 0:1]
         nc.scalar.activation(out=p[:], in_=listed[:], func=ACT.Exp, bias=neg_max[:], accum_out=p_sum)
-        v_bf = cast(1, 0, 384, 192, "v_second")
-        product(v_bf, slice(256, 384), banks[1][:, 256:], "v1_256")
-        product(v_bf, slice(0, 256), banks[1][:, :256], "v1_0")
-        last = []
-        for c0, share, tag in ((128, 0, "v_second"), (0, 128, "v_last")):
-            bank = psum.tile([P, 128], F32, name=f"last_bank{c0}")
-            product(cast(2, c0, c0 + 128, share, tag), slice(0, 128), bank[:], f"v2_{c0}")
-            last.append((slice(starts[2] + c0, starts[2] + c0 + 128), bank))
+        product(cast(2, 0, 256, 96, "v_ring"), slice(0, 256), third_bank[:], "v2")
+        product(cast(3, 0, 128, 0, "v_ring"), slice(0, 128), last_banks[0][:], "v3")
+        product(cast(3, 128, 256, 128, "v_last"), slice(0, 128), last_banks[1][:], "v4")
         inv_sum = keep.tile([P, 1], F32, align_bytes=64, tag="v_last")
         nc.vector.reciprocal(out=inv_sum[:], in_=p_sum)
 
-        dw = keep.tile([P, T], F32, tag="v_raw2")
-        nc.scalar.copy(out=dw[:, : starts[1]], in_=banks[0][:])
-        nc.vector.tensor_copy(out=dw[:, starts[1] : starts[2]], in_=banks[1][:])
-        for (cols, bank), copy in zip(last, (nc.vector.tensor_copy, nc.scalar.copy)):
-            copy(out=dw[:, cols], in_=bank[:])
+        dw = keep.tile([P, T], F32, tag="v_raw3")
+        nc.scalar.copy(out=dw[:, :512], in_=first_bank[:])
+        nc.vector.tensor_copy(out=dw[:, 512:768], in_=third_bank[:])
+        nc.vector.tensor_copy(out=dw[:, 768:896], in_=last_banks[0][:])
+        nc.scalar.copy(out=dw[:, 896:], in_=last_banks[1][:])
 
         moved = keep.tile([P, I], F32)
         nc.vector.tensor_copy(out=moved[:], in_=dw[:].indirect(lists2[:]))

from contextlib import ExitStack

import concourse.mybir as mybir

D, E, T, Q, I = 512, 512, 1024, 128, 512
FLOPS = 2 * D * Q * T + 2 * E * Q * T

F32 = mybir.dt.float32
BF16 = mybir.dt.bfloat16
I32 = mybir.dt.int32
U32 = mybir.dt.uint32
U16 = mybir.dt.uint16
U8 = mybir.dt.uint8
FP8X4 = mybir.dt.float8_e4m3fn_x4
FP4X4 = mybir.dt.float4_e2m1fn_x4
ALU = mybir.AluOpType
ACT = mybir.ActivationFunctionType

P = 128
PACK = 4
BANK = 512
CHUNKS = (256, 256, 256, 256)
PIECES = (((0, 128), (128, 384)), ((256, 384), (0, 256)), ((128, 256), (0, 128)))
SCALAR_COLS = (384, 192, 128)
OUT_CHUNKS = (256, 256, 256, 256)


def weave(copy, grouped, raw):
    copy(
        out=grouped.rearrange("p (c i t) -> p c t i", i=4, t=PACK),
        in_=raw.rearrange("p t (c i) -> p c t i", i=4),
    )


def tile_attend_gfollow_heads_kernel(tc, query, keys_words, keys_scales, gout, vals, old, offs, offs2, out):
    nc = tc.nc
    with ExitStack() as ctx:
        keep = ctx.enter_context(tc.tile_pool(name="keep", bufs=1))
        psum = ctx.enter_context(tc.psum_pool(name="psum", bufs=1))

        def quantize(bf, width, name):
            codes = keep.tile([P, width], U32, align_bytes=64, name=f"{name}_codes")
            scales = keep.tile([P, width], U8, align_bytes=64, name=f"{name}_scales")
            nc.vector.quantize_mx(out=codes[:].bitcast(FP8X4), scales=scales[:], in_=bf)
            return codes, scales

        k_scales = keep.tile([P, T], U8, align_bytes=64)
        nc.vector.memset(k_scales[:].bitcast(I32), 0)
        warm_in = keep.tile([P, 1], F32)
        nc.vector.memset(warm_in[:], 0.0)
        df = keep.tile([P, T], F32)
        nc.vector.memset(df[:], 0.0)
        warm_out = keep.tile([P, 1], F32)
        nc.scalar.activation(out=warm_out[:], in_=warm_in[:], func=ACT.Exp)

        starts = [sum(CHUNKS[:n]) for n in range(len(CHUNKS))]
        vals_by_word = vals.rearrange("(p t) c -> p t c", t=PACK)
        v_raw = [keep.tile([P, PACK, width], F32, name=f"v_raw{n}") for n, width in enumerate(CHUNKS)]

        def load_vals(n):
            nc.sync.dma_start(out=v_raw[n][:], in_=vals_by_word[:, :, starts[n] : starts[n] + CHUNKS[n]])

        lists = keep.tile([P, I // 16], U16)
        nc.sync.dma_start(lists[:], offs)
        q_raw = keep.tile([P, PACK, Q], F32)
        nc.sync.dma_start(out=q_raw[:], in_=query.rearrange("(p t) q -> p t q", t=PACK))
        k_words = keep.tile([P, 2 * T], U8, align_bytes=64)
        nc.sync.dma_start(out=k_words[:].bitcast(I32), in_=keys_words[0].bitcast(I32))
        for r in range(4):
            nc.sync.dma_start(out=k_scales[r:P:32, :].bitcast(I32), in_=keys_scales[0, r:16:4, :].bitcast(I32))
        g_raw = keep.tile([P, PACK, Q], F32)
        nc.sync.dma_start(out=g_raw[:], in_=gout.rearrange("(p t) q -> p t q", t=PACK))
        load_vals(0)
        for n in range(1, len(CHUNKS)):
            load_vals(n)
        lists2 = keep.tile([P, I // 16], U16)
        nc.sync.dma_start(lists2[:], offs2)
        old_sb = keep.tile([P, T], F32)
        nc.sync.dma_start(out=old_sb[:], in_=old)

        q_bf = keep.tile([P, PACK * Q], BF16, align_bytes=64)
        weave(nc.vector.tensor_copy, q_bf[:], q_raw[:])
        q_codes, q_scales = quantize(q_bf[:], Q, "q")
        scores = keep.tile([P, T], F32, align_bytes=64)
        c0 = 0
        for n, (width, copy) in enumerate(((512, nc.scalar.copy), (256, nc.vector.tensor_copy), (256, nc.vector.tensor_copy))):
            bank = psum.tile([P, width], F32, name=f"score_bank{n}")
            cols = slice(c0, c0 + width)
            nc.tensor.matmul_mx(
                out=bank[:],
                lhsT=q_codes[:].bitcast(FP8X4),
                lhsT_scale=q_scales[:],
                rhs=k_words[:, 2 * cols.start : 2 * cols.stop].bitcast(FP4X4),
                rhs_scale=k_scales[:, cols],
                start=True,
                stop=True,
            )
            copy(out=scores[:, cols], in_=bank[:])
            c0 = c0 + width

        g_bf = keep.tile([P, PACK * Q], BF16, align_bytes=64)
        weave(nc.vector.tensor_copy, g_bf[:], g_raw[:])
        g_codes, g_scales = quantize(g_bf[:], Q, "g")

        listed = keep.tile([P, I], F32)
        nc.vector.tensor_copy(out=listed[:], in_=scores[:].indirect(lists[:]))
        neg_max = keep.tile([P, 1], F32)
        nc.vector.tensor_reduce(out=neg_max[:], in_=listed[:], axis=mybir.AxisListType.X, op=ALU.max, negate=True)

        def cast(n, c0, c1, share, tag):
            v_bf = keep.tile([P, PACK * (c1 - c0)], BF16, align_bytes=64, name=f"v_bf{n}_{c0}", tag=tag)
            if share > 0:
                weave(nc.scalar.copy, v_bf[:, : PACK * share], v_raw[n][:, :, c0 : c0 + share])
            if c0 + share < c1:
                weave(nc.vector.tensor_copy, v_bf[:, PACK * share :], v_raw[n][:, :, c0 + share : c1])
            return v_bf

        def product(v_bf, cols, bank_cols, name):
            codes, scales = quantize(v_bf[:, PACK * cols.start : PACK * cols.stop], cols.stop - cols.start, name)
            nc.tensor.matmul_mx(
                out=bank_cols,
                lhsT=g_codes[:].bitcast(FP8X4),
                lhsT_scale=g_scales[:],
                rhs=codes[:].bitcast(FP8X4),
                rhs_scale=scales[:],
                start=True,
                stop=True,
            )

        first_bank = psum.tile([P, 512], F32)
        third_bank = psum.tile([P, 256], F32)
        last_banks = [psum.tile([P, 128], F32, name=f"last_bank{h}") for h in range(2)]
        product(cast(0, 0, 256, 256, "v_first"), slice(0, 256), first_bank[:, :256], "v0")
        product(cast(1, 0, 256, 256, "v_ring"), slice(0, 256), first_bank[:, 256:], "v1")
        p = keep.tile([P, I], F32)
        p_sum = v_raw[1][:, 0, 0:1]
        nc.scalar.activation(out=p[:], in_=listed[:], func=ACT.Exp, bias=neg_max[:], accum_out=p_sum)
        product(cast(2, 0, 256, 96, "v_ring"), slice(0, 256), third_bank[:], "v2")
        product(cast(3, 0, 128, 0, "v_ring"), slice(0, 128), last_banks[0][:], "v3")
        product(cast(3, 128, 256, 128, "v_last"), slice(0, 128), last_banks[1][:], "v4")
        inv_sum = keep.tile([P, 1], F32, align_bytes=64, tag="v_last")
        nc.vector.reciprocal(out=inv_sum[:], in_=p_sum)

        dw = keep.tile([P, T], F32, tag="v_raw3")
        nc.scalar.copy(out=dw[:, :512], in_=first_bank[:])
        nc.vector.tensor_copy(out=dw[:, 512:768], in_=third_bank[:])
        nc.vector.tensor_copy(out=dw[:, 768:896], in_=last_banks[0][:])
        nc.scalar.copy(out=dw[:, 896:], in_=last_banks[1][:])

        moved = keep.tile([P, I], F32)
        nc.vector.tensor_copy(out=moved[:], in_=dw[:].indirect(lists2[:]))
        prod = keep.tile([P, I], F32)
        mean = keep.tile([P, 1], F32)
        nc.vector.scalar_tensor_tensor(
            out=prod[:], in0=moved[:], scalar=inv_sum[:], in1=p[:], op0=ALU.mult, op1=ALU.mult, accum_out=mean[:]
        )
        centred = keep.tile([P, I], F32)
        nc.vector.tensor_scalar(
            out=centred[:], in0=moved[:], scalar1=mean[:], scalar2=inv_sum[:], op0=ALU.subtract, op1=ALU.mult
        )
        nc.vector.tensor_tensor(out=df[:].indirect(lists[:]), in0=centred[:], in1=p[:], op=ALU.mult)
        c0 = 0
        for n, width in enumerate(OUT_CHUNKS):
            res = keep.tile([P, width], F32, name=f"res{n}")
            cols = slice(c0, c0 + width)
            nc.vector.scalar_tensor_tensor(
                out=res[:], in0=df[:, cols], scalar=float(I), in1=old_sb[:, cols], op0=ALU.mult, op1=ALU.add
            )
            queue = nc.sync if n % 2 == 0 else nc.scalar
            queue.dma_start(out=out[:, cols], in_=res[:])
            c0 = c0 + width
